import numpy as np
import ml_dtypes


def mxq(x, axis, fmt="e4m3"):
    dtype, down = {"e4m3": (ml_dtypes.float8_e4m3fn, 7), "e5m2": (ml_dtypes.float8_e5m2, 14)}[fmt]
    v = np.moveaxis(np.asarray(x, np.float32).astype(ml_dtypes.bfloat16).astype(np.float64), axis, -1)
    blocks = v.reshape(v.shape[:-1] + (-1, 32))
    amax = np.abs(blocks).max(-1, keepdims=True)
    byte = np.maximum(np.where(amax > 0, np.frexp(amax)[1] - 1 + 127, 0) - down, 1)
    scale = np.exp2(byte - 127.0)
    codes = (blocks / scale).astype(np.float32).astype(dtype).astype(np.float64)
    return np.moveaxis((codes * scale).reshape(v.shape), -1, axis)


WIDE = False


def mx_kscale(k):
    if not WIDE:
        return np.ones(k)
    levels = np.array([10, -10, 5, -5, 0])
    if k % 512:
        return np.exp2(np.random.permutation(np.resize(levels, k // 32))).repeat(32)
    a = np.empty((k // 512, 16))
    for p in range(k // 512):
        a[p, :8] = np.random.permutation(np.resize(levels, 8))
        for g in range(8):
            far = levels[np.abs(levels - a[p, g]) >= 10]
            a[p, g + 8] = far[np.random.randint(len(far))]
    return np.exp2(a.ravel()).repeat(32)


def f64(x):
    return np.asarray(x).astype(np.float64)


def striped(idx):
    return np.tile(idx.reshape(-1, 16).T, (8, 1)).astype(np.uint16)


def unstriped(offs):
    return offs[:16].T.reshape(-1).astype(np.int64)


def pack_weight(w):
    k, n = w.shape
    w = f64(np.asarray(w, np.float32).astype(ml_dtypes.bfloat16)).reshape(k // 32, 32, n)
    amax = np.abs(w).max(1)
    byte = np.clip(np.where(amax > 0, np.frexp(amax)[1] - 1 + 127 - 7, 1), 1, 254)
    scaled = (w * np.exp2(127.0 - byte)[:, None, :]).reshape(k, n).astype(np.float32)
    words = np.ascontiguousarray(scaled.reshape(k // 512, 128, 4, n).transpose(0, 1, 3, 2)).astype(ml_dtypes.float8_e4m3fn).view(np.uint8)
    return words, np.ascontiguousarray(byte.astype(np.uint8).reshape(k // 512, 16, n))


def unpack_weight(words, scales):
    g, p, n, _ = words.shape
    vals = np.ascontiguousarray(words).view(ml_dtypes.float8_e4m3fn).astype(np.float64) * np.repeat(np.exp2(scales.astype(np.float64) - 127.0), 8, axis=1)[..., None]
    return vals.transpose(0, 1, 3, 2).reshape(g * 512, n)


def relu(v):
    return np.maximum(v, 0.0)


K, T, S, V, H, N = 512, 4096, 1536, 512, 512, 256


def setup_inputs():
    n = np.random.standard_normal
    s = mx_kscale(K)[:, None]
    u = mx_kscale(H)
    packed_xT = pack_weight(n((K, T)) * s)
    packed_w4 = pack_weight(n((H, N)) / np.sqrt(H) / u[:, None])
    return {
        "x_words": packed_xT[0],
        "x_scales": packed_xT[1],
        "w1": (n((K, H)) / np.sqrt(K) / s * u).astype(np.float32),
        "w2": (n((K, H)) / np.sqrt(K) / s).astype(np.float32),
        "w3": (n((K, H)) / np.sqrt(K) / s).astype(np.float32),
        "w4_words": packed_w4[0],
        "w4_scales": packed_w4[1],
        "offs": striped(np.random.permutation(T)[:S]),
    }


def reference(x_words, x_scales, w1, w2, w3, w4_words, w4_scales, offs):
    xq = unpack_weight(x_words, x_scales)[:, unstriped(offs)]
    z = (((mxq(f64(w1), 0, "e4m3").T @ xq[:, :V])) * ((mxq(f64(w2), 0, "e4m3").T @ xq[:, V:2 * V]))) * ((mxq(f64(w3), 0, "e4m3").T @ xq[:, 2 * V:3 * V]))
    return relu(unpack_weight(w4_words, w4_scales).T @ mxq(z, 0, "e4m3"))

@@ -1,0 +1,167 @@
+from contextlib import ExitStack
+
+import concourse.mybir as mybir
+
+K, T, S, V, H, N = 512, 4096, 1536, 512, 512, 256
+FLOPS = 2 * 3 * K * H * V + 2 * H * N * V
+
+F32 = mybir.dt.float32
+BF16 = mybir.dt.bfloat16
+I32 = mybir.dt.int32
+U32 = mybir.dt.uint32
+U16 = mybir.dt.uint16
+U8 = mybir.dt.uint8
+FP8X4 = mybir.dt.float8_e4m3fn_x4
+MULT = mybir.AluOpType.mult
+ADD = mybir.AluOpType.add
+RELU = mybir.ActivationFunctionType.Relu
+
+P = 128
+PACK = 4
+CHUNK = 128
+CHUNKS = V // CHUNK
+
+
+def tile_picked_trilin_relu_p_kernel(
+    tc, x_words, x_scales, w1, w2, w3, w4_words, w4_scales, offs, out
+):
+    nc = tc.nc
+    with ExitStack() as ctx:
+        keep = ctx.enter_context(tc.tile_pool(name="keep", bufs=1))
+        psum = ctx.enter_context(tc.psum_pool(name="psum", bufs=8))
+
+        def tile(shape, dtype, name):
+            return keep.tile(shape, dtype, name=name, align_bytes=64)
+
+        offsets = keep.tile([P, S // 16], U16, name="offsets")
+        table_words = tile([P, T], I32, "table_words")
+        table_scales = tile([P, T], U8, "table_scales")
+        raw = [tile([P, PACK, H], F32, f"raw{d}") for d in range(3)]
+        w4_codes = tile([P, N], I32, "w4_codes")
+        w4_plane = tile([P, N], U8, "w4_plane")
+
+        def load_scale_rows(plane, rows):
+            for r in range(4):
+                nc.sync.dma_start(out=plane[r:P:32, :].bitcast(I32), in_=rows[r:16:4, :].bitcast(I32))
+
+        def load_weight(d, w):
+            nc.sync.dma_start(out=raw[d][:], in_=w.rearrange("(p j) c -> p j c", j=PACK))
+
+        nc.vector.memset(table_scales[:].bitcast(I32), 0)
+        nc.vector.memset(w4_plane[:].bitcast(I32), 0)
+        load_weight(0, w1)
+        nc.sync.dma_start(offsets[:], offs)
+        load_scale_rows(table_scales, x_scales[0])
+        nc.sync.dma_start(out=table_words[:], in_=x_words[0].rearrange("p n t -> p (n t)").bitcast(I32))
+        load_weight(1, w2)
+        load_weight(2, w3)
+        nc.sync.dma_start(out=w4_codes[:], in_=w4_words[0].rearrange("p n t -> p (n t)").bitcast(I32))
+        load_scale_rows(w4_plane, w4_scales[0])
+
+        def cast(engine, d, dst, t0, t1, m0=0, m1=P):
+            src = raw[d][:].rearrange("p j (m t) -> p m j t", t=PACK)[:, m0:m1, :, t0:t1]
+            dst = dst[:].rearrange("p t m j -> p m j t")[:, m0:m1, :, t0:t1]
+            if engine == "scalar":
+                nc.scalar.copy(out=dst, in_=src)
+            elif engine == "vector":
+                nc.vector.tensor_copy(out=dst, in_=src)
+            else:
+                nc.gpsimd.tensor_scalar(dst, src, 1.0, 0.0, MULT, ADD)
+
+        def quantize(codes, plane, src, t0, t1):
+            nc.vector.quantize_mx(
+                out=codes[:, t0 * P : t1 * P].bitcast(FP8X4),
+                scales=plane[:, t0 * P : t1 * P],
+                in_=src[:, t0:t1].rearrange("p t m j -> p (t m j)"),
+            )
+
+        def gather_words(dst, d):
+            piece = offsets[:, d * V // 16 : (d + 1) * V // 16]
+            nc.vector.tensor_copy(dst[:], table_words[:].bitcast(U32).indirect(piece))
+
+        def product(codes, plane, words, d, c):
+            bank = psum.tile([P, PACK, CHUNK], F32, name="bank")
+            cols = slice(c * CHUNK, (c + 1) * CHUNK)
+            for t in range(PACK):
+                m = slice(t * P, (t + 1) * P)
+                nc.tensor.matmul_mx(
+                    out=bank[:, t, :],
+                    lhsT=codes[:, m].bitcast(FP8X4),
+                    lhsT_scale=plane[:, m],
+                    rhs=words[:, cols].bitcast(FP8X4),
+                    rhs_scale=picked_scales[:, d * V + c * CHUNK : d * V + (c + 1) * CHUNK],
+                    start=True,
+                    stop=True,
+                )
+            return bank[:].rearrange("p t v -> p v t")
+
+        picked_scales = tile([P, S], U8, "picked_scales")
+        g1 = tile([P, PACK, P, PACK], BF16, "g1")
+        g2 = tile([P, PACK, P, PACK], BF16, "g2")
+        g3 = tile([P, PACK, P, PACK], BF16, "g3")
+        s1 = tile([P, H], U8, "s1")
+        s2 = tile([P, H], U8, "s2")
+        s3 = tile([P, H], U8, "s3")
+        q2 = tile([P, H], U32, "q2")
+        q3 = tile([P, H], U32, "q3")
+        x1 = tile([P, V], U32, "x1")
+        x2 = tile([P, V], U32, "x2")
+        y1 = [tile([P, CHUNK, PACK], F32, f"y1_{c}") for c in range(CHUNKS)]
+        z = [tile([P, CHUNK, PACK], BF16, f"z_{c}") for c in range(CHUNKS)]
+        z_codes = [tile([P, CHUNK], U32, f"z_codes{c}") for c in range(CHUNKS)]
+        z_plane = [tile([P, CHUNK], U8, f"z_plane{c}") for c in range(CHUNKS)]
+        result = [tile([P, N // P, CHUNK], F32, f"result{c}") for c in range(CHUNKS)]
+
+
+        cast("scalar", 0, g1, 0, 4)
+        nc.vector.tensor_copy(picked_scales[:], table_scales[:].indirect(offsets[:]))
+        q1 = tile([P, H], U32, "table_scales")
+        quantize(q1, s1, g1, 0, 4)
+        gather_words(x1, 0)
+        gather_words(x2, 1)
+        for c in range(CHUNKS):
+            nc.scalar.copy(out=y1[c][:], in_=product(q1, s1, x1, 0, c))
+        cast("vector", 1, g2, 0, 2)
+        cast("vector", 1, g2, 2, 4)
+        quantize(q2, s2, g2, 0, 2)
+        quantize(q2, s2, g2, 2, 4)
+        x3 = tile([P, V], U32, "g2")
+        gather_words(x3, 2)
+        cast("scalar", 2, g3, 0, 4, 0, 108)
+        cast("vector", 2, g3, 0, 4, 108, P)
+        early = tile([P, 2, CHUNK, PACK], F32, "early")
+        for c in range(2):
+            nc.vector.tensor_tensor(early[:, c], product(q2, s2, x2, 1, c), y1[c][:], MULT)
+        quantize(q3, s3, g3, 0, 4)
+        late = tile([P, 2, CHUNK, PACK], F32, "g3")
+        for c in range(2, CHUNKS):
+            nc.vector.tensor_tensor(late[:, c - 2], product(q2, s2, x2, 1, c), y1[c][:], MULT)
+        y12 = [early[:, 0], early[:, 1], late[:, 0], late[:, 1]]
+
+
+        def finish(c):
+            nc.vector.quantize_mx(
+                out=z_codes[c][:].bitcast(FP8X4), scales=z_plane[c][:], in_=z[c][:].rearrange("p v t -> p (v t)")
+            )
+            bank = psum.tile([P, PACK, CHUNK], F32, name="bank")
+            for h in range(N // P):
+                m = slice(h * P, (h + 1) * P)
+                nc.tensor.matmul_mx(
+                    out=bank[:, h, :],
+                    lhsT=w4_codes[:, m].bitcast(FP8X4),
+                    lhsT_scale=w4_plane[:, m],
+                    rhs=z_codes[c][:].bitcast(FP8X4),
+                    rhs_scale=z_plane[c][:],
+                    start=True,
+                    stop=True,
+                )
+            nc.scalar.activation(out=result[c][:], in_=bank[:, : N // P, :], func=RELU)
+            nc.sync.dma_start(
+                out=out[:, c * CHUNK : (c + 1) * CHUNK].rearrange("(h p) v -> p h v", p=P), in_=result[c][:]
+            )
+
+        for c in range(CHUNKS):
+            nc.vector.tensor_tensor(z[c][:], product(q3, s3, x3, 2, c), y12[c], MULT)
+            if c > 0:
+                finish(c - 1)
+        finish(CHUNKS - 1)

@@ -13,13 +13,17 @@ U16 = mybir.dt.uint16
 U8 = mybir.dt.uint8
 FP8X4 = mybir.dt.float8_e4m3fn_x4
 MULT = mybir.AluOpType.mult
-ADD = mybir.AluOpType.add
 RELU = mybir.ActivationFunctionType.Relu
 
 P = 128
 PACK = 4
+BLOCKS = K // 32
 CHUNK = 128
 CHUNKS = V // CHUNK
+PSUM_BANKS = 8
+TABLE_HEAD = 1024
+SCALAR_W3_SHARE = 48
+PIECES = ((0, 128), (128, 256), (256, 384), (384, 448), (448, 512))
 
 
 def tile_picked_trilin_relu_p_kernel(
@@ -28,10 +32,10 @@ def tile_picked_trilin_relu_p_kernel(
     nc = tc.nc
     with ExitStack() as ctx:
         keep = ctx.enter_context(tc.tile_pool(name="keep", bufs=1))
-        psum = ctx.enter_context(tc.psum_pool(name="psum", bufs=8))
+        psum = ctx.enter_context(tc.psum_pool(name="psum", bufs=PSUM_BANKS))
 
-        def tile(shape, dtype, name):
-            return keep.tile(shape, dtype, name=name, align_bytes=64)
+        def tile(shape, dtype, slot):
+            return keep.tile(shape, dtype, name=slot, align_bytes=64)
 
         offsets = keep.tile([P, S // 16], U16, name="offsets")
         table_words = tile([P, T], I32, "table_words")
@@ -39,129 +43,147 @@ def tile_picked_trilin_relu_p_kernel(
         raw = [tile([P, PACK, H], F32, f"raw{d}") for d in range(3)]
         w4_codes = tile([P, N], I32, "w4_codes")
         w4_plane = tile([P, N], U8, "w4_plane")
-
-        def load_scale_rows(plane, rows):
-            for r in range(4):
-                nc.sync.dma_start(out=plane[r:P:32, :].bitcast(I32), in_=rows[r:16:4, :].bitcast(I32))
-
-        def load_weight(d, w):
-            nc.sync.dma_start(out=raw[d][:], in_=w.rearrange("(p j) c -> p j c", j=PACK))
+        spread_scales = tile([P, S], U8, "spread_scales")
+        picked_scales = tile([P, S], U8, "picked_scales")
 
         nc.vector.memset(table_scales[:].bitcast(I32), 0)
         nc.vector.memset(w4_plane[:].bitcast(I32), 0)
-        load_weight(0, w1)
+        nc.vector.memset(picked_scales[:].bitcast(I32), 0)
+        words_hbm = x_words[0].rearrange("p n j -> p (n j)").bitcast(I32)
+        w_rows = [w.rearrange("(p j) i -> p j i", j=PACK) for w in (w1, w2, w3)]
         nc.sync.dma_start(offsets[:], offs)
-        load_scale_rows(table_scales, x_scales[0])
-        nc.sync.dma_start(out=table_words[:], in_=x_words[0].rearrange("p n t -> p (n t)").bitcast(I32))
-        load_weight(1, w2)
-        load_weight(2, w3)
-        nc.sync.dma_start(out=w4_codes[:], in_=w4_words[0].rearrange("p n t -> p (n t)").bitcast(I32))
-        load_scale_rows(w4_plane, w4_scales[0])
+        nc.sync.dma_start(out=table_words[:, :TABLE_HEAD], in_=words_hbm[:, :TABLE_HEAD])
+        nc.sync.dma_start(out=table_scales[0 : P : P // BLOCKS, :].bitcast(I32), in_=x_scales[0].bitcast(I32))
+        nc.sync.dma_start(out=raw[0][:], in_=w_rows[0])
+        nc.sync.dma_start(out=table_words[:, TABLE_HEAD:], in_=words_hbm[:, TABLE_HEAD:])
+        nc.sync.dma_start(out=raw[1][:, :2], in_=w_rows[1][:, :2])
+        nc.vector.tensor_copy(spread_scales[:], table_scales[:].indirect(offsets[:]))
+        for r in range(4):
+            nc.sync.dma_start(
+                out=picked_scales[r:P:32, :].bitcast(I32), in_=spread_scales[8 * r : P : 32, :].bitcast(I32)
+            )
+        nc.sync.dma_start(out=raw[1][:, 2:], in_=w_rows[1][:, 2:])
+        nc.sync.dma_start(out=raw[2][:], in_=w_rows[2])
+        nc.sync.dma_start(out=w4_codes[:], in_=w4_words[0].rearrange("p n j -> p (n j)").bitcast(I32))
+        for r in range(4):
+            nc.sync.dma_start(out=w4_plane[r:P:32, :].bitcast(I32), in_=w4_scales[0, r:BLOCKS:4, :].bitcast(I32))
 
-        def cast(engine, d, dst, t0, t1, m0=0, m1=P):
-            src = raw[d][:].rearrange("p j (m t) -> p m j t", t=PACK)[:, m0:m1, :, t0:t1]
-            dst = dst[:].rearrange("p t m j -> p m j t")[:, m0:m1, :, t0:t1]
-            if engine == "scalar":
-                nc.scalar.copy(out=dst, in_=src)
-            elif engine == "vector":
-                nc.vector.tensor_copy(out=dst, in_=src)
-            else:
-                nc.gpsimd.tensor_scalar(dst, src, 1.0, 0.0, MULT, ADD)
+        def half_tile(slot):
+            return tile([P, 2, P, PACK], BF16, slot)
 
-        def quantize(codes, plane, src, t0, t1):
+        def round_weight(copy, d, rounded, half, ms=slice(0, P), js=slice(0, PACK)):
+            src = raw[d][:].rearrange("p j (m t) -> p m j t", t=PACK)[:, ms, js, 2 * half : 2 * half + 2]
+            copy(out=rounded[half][:].rearrange("p t m j -> p m j t")[:, ms, js, :], in_=src)
+
+        def quantize_half(codes, plane, rounded, half):
+            cols = slice(2 * half * P, (2 * half + 2) * P)
             nc.vector.quantize_mx(
-                out=codes[:, t0 * P : t1 * P].bitcast(FP8X4),
-                scales=plane[:, t0 * P : t1 * P],
-                in_=src[:, t0:t1].rearrange("p t m j -> p (t m j)"),
+                out=codes[:, cols].bitcast(FP8X4),
+                scales=plane[:, cols],
+                in_=rounded[half][:].rearrange("p t m j -> p (t m j)"),
             )
 
-        def gather_words(dst, d):
+        def gather_words(picked, d):
             piece = offsets[:, d * V // 16 : (d + 1) * V // 16]
-            nc.vector.tensor_copy(dst[:], table_words[:].bitcast(U32).indirect(piece))
+            nc.vector.tensor_copy(picked, table_words[:].bitcast(U32).indirect(piece))
 
-        def product(codes, plane, words, d, c):
+        def product(codes, plane, picked, d, c):
             bank = psum.tile([P, PACK, CHUNK], F32, name="bank")
-            cols = slice(c * CHUNK, (c + 1) * CHUNK)
             for t in range(PACK):
-                m = slice(t * P, (t + 1) * P)
+                cols = slice(t * P, (t + 1) * P)
                 nc.tensor.matmul_mx(
                     out=bank[:, t, :],
-                    lhsT=codes[:, m].bitcast(FP8X4),
-                    lhsT_scale=plane[:, m],
-                    rhs=words[:, cols].bitcast(FP8X4),
+                    lhsT=codes[:, cols].bitcast(FP8X4),
+                    lhsT_scale=plane[:, cols],
+                    rhs=picked[:, c * CHUNK : (c + 1) * CHUNK].bitcast(FP8X4),
                     rhs_scale=picked_scales[:, d * V + c * CHUNK : d * V + (c + 1) * CHUNK],
                     start=True,
                     stop=True,
                 )
             return bank[:].rearrange("p t v -> p v t")
 
-        picked_scales = tile([P, S], U8, "picked_scales")
-        g1 = tile([P, PACK, P, PACK], BF16, "g1")
-        g2 = tile([P, PACK, P, PACK], BF16, "g2")
-        g3 = tile([P, PACK, P, PACK], BF16, "g3")
-        s1 = tile([P, H], U8, "s1")
-        s2 = tile([P, H], U8, "s2")
-        s3 = tile([P, H], U8, "s3")
-        q2 = tile([P, H], U32, "q2")
-        q3 = tile([P, H], U32, "q3")
-        x1 = tile([P, V], U32, "x1")
-        x2 = tile([P, V], U32, "x2")
-        y1 = [tile([P, CHUNK, PACK], F32, f"y1_{c}") for c in range(CHUNKS)]
-        z = [tile([P, CHUNK, PACK], BF16, f"z_{c}") for c in range(CHUNKS)]
-        z_codes = [tile([P, CHUNK], U32, f"z_codes{c}") for c in range(CHUNKS)]
-        z_plane = [tile([P, CHUNK], U8, f"z_plane{c}") for c in range(CHUNKS)]
-        result = [tile([P, N // P, CHUNK], F32, f"result{c}") for c in range(CHUNKS)]
+        def chunk_tile(slot):
+            return tile([P, CHUNK, PACK], F32, slot)
 
+        planes = [tile([P, H], U8, f"plane{d}") for d in range(3)]
 
-        cast("scalar", 0, g1, 0, 4)
-        nc.vector.tensor_copy(picked_scales[:], table_scales[:].indirect(offsets[:]))
-        q1 = tile([P, H], U32, "table_scales")
-        quantize(q1, s1, g1, 0, 4)
-        gather_words(x1, 0)
-        gather_words(x2, 1)
+        rounded1 = [half_tile("rounded1a"), half_tile("rounded1b")]
+        rounded2 = [half_tile("rounded2a"), half_tile("rounded2b")]
+        codes1 = tile([P, H], U32, "table_scales")
+        for half in range(2):
+            round_weight(nc.scalar.copy, 0, rounded1, half)
+        for half in range(2):
+            quantize_half(codes1, planes[0], rounded1, half)
+        picked12 = tile([P, 2, V], U32, "rounded1b")
+        gather_words(picked12[:, 0], 0)
+        gather_words(picked12[:, 1], 1)
+        for half in range(2):
+            round_weight(nc.scalar.copy, 1, rounded2, half, js=slice(0, 2))
+        y1 = [chunk_tile(f"y1_{c}") for c in range(CHUNKS)]
         for c in range(CHUNKS):
-            nc.scalar.copy(out=y1[c][:], in_=product(q1, s1, x1, 0, c))
-        cast("vector", 1, g2, 0, 2)
-        cast("vector", 1, g2, 2, 4)
-        quantize(q2, s2, g2, 0, 2)
-        quantize(q2, s2, g2, 2, 4)
-        x3 = tile([P, V], U32, "g2")
-        gather_words(x3, 2)
-        cast("scalar", 2, g3, 0, 4, 0, 108)
-        cast("vector", 2, g3, 0, 4, 108, P)
-        early = tile([P, 2, CHUNK, PACK], F32, "early")
+            nc.scalar.copy(out=y1[c][:], in_=product(codes1, planes[0], picked12[:, 0], 0, c))
+
+        codes2 = tile([P, H], U32, "codes2")
+        for half in range(2):
+            round_weight(nc.vector.tensor_copy, 1, rounded2, half, js=slice(2, PACK))
+        for half in range(2):
+            quantize_half(codes2, planes[1], rounded2, half)
+        picked3 = tile([P, V], U32, "rounded2a")
+        gather_words(picked3[:], 2)
+
+        def second_factor(c):
+            return product(codes2, planes[1], picked12[:, 1], 1, c)
+
+        rounded3 = [half_tile("rounded3a"), half_tile("rounded3b")]
+        codes3 = tile([P, H], U32, "codes3")
+        round_weight(nc.scalar.copy, 2, rounded3, 0)
+        round_weight(nc.scalar.copy, 2, rounded3, 1, ms=slice(0, SCALAR_W3_SHARE))
+        round_weight(nc.vector.tensor_copy, 2, rounded3, 1, ms=slice(SCALAR_W3_SHARE, P))
+        y12 = [chunk_tile("y12_0")[:], chunk_tile("y12_1")[:]]
         for c in range(2):
-            nc.vector.tensor_tensor(early[:, c], product(q2, s2, x2, 1, c), y1[c][:], MULT)
-        quantize(q3, s3, g3, 0, 4)
-        late = tile([P, 2, CHUNK, PACK], F32, "g3")
-        for c in range(2, CHUNKS):
-            nc.vector.tensor_tensor(late[:, c - 2], product(q2, s2, x2, 1, c), y1[c][:], MULT)
-        y12 = [early[:, 0], early[:, 1], late[:, 0], late[:, 1]]
+            nc.vector.tensor_tensor(y12[c], second_factor(c), y1[c][:], MULT)
+        for half in range(2):
+            quantize_half(codes3, planes[2], rounded3, half)
+        y12_late = tile([P, 2, CHUNK, PACK], F32, "rounded3b")
+        y12.extend([y12_late[:, 0], y12_late[:, 1]])
+        nc.vector.tensor_tensor(y12[2], second_factor(2), y1[2][:], MULT)
+        y2_last = chunk_tile("raw2")
+        nc.scalar.copy(out=y2_last[:], in_=second_factor(3))
+        nc.gpsimd.tensor_tensor(y12[3], y2_last[:], y1[3][:], MULT)
 
+        z = tile([P, V, PACK], BF16, "z")
+        y3 = [product(codes3, planes[2], picked3, 2, c) for c in range(CHUNKS)]
 
-        def finish(c):
+        def multiply_piece(v0, v1):
+            c, first = divmod(v0, CHUNK)
+            inside = slice(first, first + v1 - v0)
+            nc.vector.tensor_tensor(z[:, v0:v1], y3[c][:, inside], y12[c][:, inside], MULT)
+
+        def finish_piece(v0, v1):
+            width = v1 - v0
+            z_codes = tile([P, width], U32, f"z_codes{v0}")
+            z_plane = tile([P, width], U8, f"z_plane{v0}")
+            result = tile([P, N // P, width], F32, f"result{v0}")
             nc.vector.quantize_mx(
-                out=z_codes[c][:].bitcast(FP8X4), scales=z_plane[c][:], in_=z[c][:].rearrange("p v t -> p (v t)")
+                out=z_codes[:].bitcast(FP8X4), scales=z_plane[:], in_=z[:, v0:v1].rearrange("p v t -> p (v t)")
             )
             bank = psum.tile([P, PACK, CHUNK], F32, name="bank")
             for h in range(N // P):
-                m = slice(h * P, (h + 1) * P)
+                cols = slice(h * P, (h + 1) * P)
                 nc.tensor.matmul_mx(
-                    out=bank[:, h, :],
-                    lhsT=w4_codes[:, m].bitcast(FP8X4),
-                    lhsT_scale=w4_plane[:, m],
-                    rhs=z_codes[c][:].bitcast(FP8X4),
-                    rhs_scale=z_plane[c][:],
+                    out=bank[:, h, :width],
+                    lhsT=w4_codes[:, cols].bitcast(FP8X4),
+                    lhsT_scale=w4_plane[:, cols],
+                    rhs=z_codes[:].bitcast(FP8X4),
+                    rhs_scale=z_plane[:],
                     start=True,
                     stop=True,
                 )
-            nc.scalar.activation(out=result[c][:], in_=bank[:, : N // P, :], func=RELU)
-            nc.sync.dma_start(
-                out=out[:, c * CHUNK : (c + 1) * CHUNK].rearrange("(h p) v -> p h v", p=P), in_=result[c][:]
-            )
+            nc.scalar.activation(out=result[:], in_=bank[:, : N // P, :width], func=RELU)
+            nc.sync.dma_start(out=out[:, v0:v1].rearrange("(h p) v -> p h v", p=P), in_=result[:])
 
-        for c in range(CHUNKS):
-            nc.vector.tensor_tensor(z[c][:], product(q3, s3, x3, 2, c), y12[c], MULT)
-            if c > 0:
-                finish(c - 1)
-        finish(CHUNKS - 1)
+        for before, piece in zip((None,) + PIECES, PIECES + (None,)):
+            if piece is not None:
+                multiply_piece(*piece)
+            if before is not None:
+                finish_piece(*before)

@@ -13,6 +13,7 @@ U16 = mybir.dt.uint16
 U8 = mybir.dt.uint8
 FP8X4 = mybir.dt.float8_e4m3fn_x4
 MULT = mybir.AluOpType.mult
+ADD = mybir.AluOpType.add
 RELU = mybir.ActivationFunctionType.Relu
 
 P = 128
@@ -22,7 +23,7 @@ CHUNK = 128
 CHUNKS = V // CHUNK
 PSUM_BANKS = 8
 TABLE_HEAD = 1024
-SCALAR_W3_SHARE = 48
+SCALAR_W3_SHARE = 32
 PIECES = ((0, 128), (128, 256), (256, 384), (384, 448), (448, 512))
 
 
@@ -74,6 +75,11 @@ def tile_picked_trilin_relu_p_kernel(
         def round_weight(copy, d, rounded, half, ms=slice(0, P), js=slice(0, PACK)):
             src = raw[d][:].rearrange("p j (m t) -> p m j t", t=PACK)[:, ms, js, 2 * half : 2 * half + 2]
             copy(out=rounded[half][:].rearrange("p t m j -> p m j t")[:, ms, js, :], in_=src)
+
+        def gpsimd_round(out, in_):
+            nc.gpsimd.tensor_scalar(
+                out.rearrange("p m j t -> p m t j"), in_.rearrange("p m j t -> p m t j"), 1.0, 0.0, MULT, ADD
+            )
 
         def quantize_half(codes, plane, rounded, half):
             cols = slice(2 * half * P, (2 * half + 2) * P)
@@ -138,7 +144,7 @@ def tile_picked_trilin_relu_p_kernel(
         codes3 = tile([P, H], U32, "codes3")
         round_weight(nc.scalar.copy, 2, rounded3, 0)
         round_weight(nc.scalar.copy, 2, rounded3, 1, ms=slice(0, SCALAR_W3_SHARE))
-        round_weight(nc.vector.tensor_copy, 2, rounded3, 1, ms=slice(SCALAR_W3_SHARE, P))
+        round_weight(gpsimd_round, 2, rounded3, 1, ms=slice(SCALAR_W3_SHARE, P))
         y12 = [chunk_tile("y12_0")[:], chunk_tile("y12_1")[:]]
         for c in range(2):
             nc.vector.tensor_tensor(y12[c], second_factor(c), y1[c][:], MULT)
@@ -180,7 +186,8 @@ def tile_picked_trilin_relu_p_kernel(
                     stop=True,
                 )
             nc.scalar.activation(out=result[:], in_=bank[:, : N // P, :width], func=RELU)
-            nc.sync.dma_start(out=out[:, v0:v1].rearrange("(h p) v -> p h v", p=P), in_=result[:])
+            queue = nc.scalar if v1 == V else nc.sync
+            queue.dma_start(out=out[:, v0:v1].rearrange("(h p) v -> p h v", p=P), in_=result[:])
 
         for before, piece in zip((None,) + PIECES, PIECES + (None,)):
             if piece is not None:

@@ -150,12 +150,12 @@ def tile_picked_trilin_relu_p_kernel(
             nc.vector.tensor_tensor(y12[c], second_factor(c), y1[c][:], MULT)
         for half in range(2):
             quantize_half(codes3, planes[2], rounded3, half)
-        y12_late = tile([P, 2, CHUNK, PACK], F32, "rounded3b")
-        y12.extend([y12_late[:, 0], y12_late[:, 1]])
+        after_rounding = tile([P, 2, CHUNK, PACK], F32, "raw2")
+        y2_last = after_rounding[:, 1]
+        y12.extend([after_rounding[:, 0], chunk_tile("rounded3b")[:]])
         nc.vector.tensor_tensor(y12[2], second_factor(2), y1[2][:], MULT)
-        y2_last = chunk_tile("raw2")
-        nc.scalar.copy(out=y2_last[:], in_=second_factor(3))
-        nc.gpsimd.tensor_tensor(y12[3], y2_last[:], y1[3][:], MULT)
+        nc.scalar.copy(out=y2_last, in_=second_factor(3))
+        nc.gpsimd.tensor_tensor(y12[3], y2_last, y1[3][:], MULT)
 
         z = tile([P, V, PACK], BF16, "z")
         y3 = [product(codes3, planes[2], picked3, 2, c) for c in range(CHUNKS)]

@@ -52,16 +52,16 @@ def tile_picked_trilin_relu_p_kernel(
         nc.vector.memset(picked_scales[:].bitcast(I32), 0)
         words_hbm = x_words[0].rearrange("p n j -> p (n j)").bitcast(I32)
         w_rows = [w.rearrange("(p j) i -> p j i", j=PACK) for w in (w1, w2, w3)]
-        nc.sync.dma_start(offsets[:], offs)
         nc.sync.dma_start(out=table_words[:, :TABLE_HEAD], in_=words_hbm[:, :TABLE_HEAD])
-        nc.sync.dma_start(out=table_scales[0 : P : P // BLOCKS, :].bitcast(I32), in_=x_scales[0].bitcast(I32))
+        nc.sync.dma_start(offsets[:], offs)
+        nc.sync.dma_start(out=table_scales[4 : P : P // BLOCKS, :].bitcast(I32), in_=x_scales[0].bitcast(I32))
         nc.sync.dma_start(out=raw[0][:], in_=w_rows[0])
         nc.sync.dma_start(out=table_words[:, TABLE_HEAD:], in_=words_hbm[:, TABLE_HEAD:])
         nc.sync.dma_start(out=raw[1][:, :2], in_=w_rows[1][:, :2])
         nc.vector.tensor_copy(spread_scales[:], table_scales[:].indirect(offsets[:]))
         for r in range(4):
             nc.sync.dma_start(
-                out=picked_scales[r:P:32, :].bitcast(I32), in_=spread_scales[8 * r : P : 32, :].bitcast(I32)
+                out=picked_scales[r:P:32, :].bitcast(I32), in_=spread_scales[8 * r + 4 : P : 32, :].bitcast(I32)
             )
         nc.sync.dma_start(out=raw[1][:, 2:], in_=w_rows[1][:, 2:])
         nc.sync.dma_start(out=raw[2][:], in_=w_rows[2])

@@ -54,17 +54,23 @@ def tile_picked_trilin_relu_p_kernel(
         w_rows = [w.rearrange("(p j) i -> p j i", j=PACK) for w in (w1, w2, w3)]
         nc.sync.dma_start(out=table_words[:, :TABLE_HEAD], in_=words_hbm[:, :TABLE_HEAD])
         nc.sync.dma_start(offsets[:], offs)
-        nc.sync.dma_start(out=table_scales[4 : P : P // BLOCKS, :].bitcast(I32), in_=x_scales[0].bitcast(I32))
+        nc.sync.dma_start(out=table_scales[11 : 11 + 7 * BLOCKS : 7, :].bitcast(I32), in_=x_scales[0].bitcast(I32))
         nc.sync.dma_start(out=raw[0][:], in_=w_rows[0])
         nc.sync.dma_start(out=table_words[:, TABLE_HEAD:], in_=words_hbm[:, TABLE_HEAD:])
         nc.sync.dma_start(out=raw[1][:, :2], in_=w_rows[1][:, :2])
         nc.vector.tensor_copy(spread_scales[:], table_scales[:].indirect(offsets[:]))
-        for r in range(4):
-            nc.sync.dma_start(
-                out=picked_scales[r:P:32, :].bitcast(I32), in_=spread_scales[8 * r + 4 : P : 32, :].bitcast(I32)
-            )
+
+        def move_scales(cols):
+            for r in range(4):
+                nc.sync.dma_start(
+                    out=picked_scales[r:P:32, cols].bitcast(I32),
+                    in_=spread_scales[11 + 7 * r : 11 + 7 * BLOCKS : 28, cols].bitcast(I32),
+                )
+
+        move_scales(slice(0, 2 * V))
         nc.sync.dma_start(out=raw[1][:, 2:], in_=w_rows[1][:, 2:])
         nc.sync.dma_start(out=raw[2][:], in_=w_rows[2])
+        move_scales(slice(2 * V, S))
         nc.sync.dma_start(out=w4_codes[:], in_=w4_words[0].rearrange("p n j -> p (n j)").bitcast(I32))
         for r in range(4):
             nc.sync.dma_start(out=w4_plane[r:P:32, :].bitcast(I32), in_=w4_scales[0, r:BLOCKS:4, :].bitcast(I32))

@@ -23,7 +23,7 @@ CHUNK = 128
 CHUNKS = V // CHUNK
 PSUM_BANKS = 8
 TABLE_HEAD = 1024
-SCALAR_W3_SHARE = 32
+SCALAR_W3_SHARE = 48
 PIECES = ((0, 128), (128, 256), (256, 384), (384, 448), (448, 512))
 
 
@@ -88,10 +88,9 @@ def tile_picked_trilin_relu_p_kernel(
             )
 
         def quantize_half(codes, plane, rounded, half):
-            cols = slice(2 * half * P, (2 * half + 2) * P)
             nc.vector.quantize_mx(
-                out=codes[:, cols].bitcast(FP8X4),
-                scales=plane[:, cols],
+                out=codes[half].bitcast(FP8X4),
+                scales=plane[half],
                 in_=rounded[half][:].rearrange("p t m j -> p (t m j)"),
             )
 
@@ -102,11 +101,11 @@ def tile_picked_trilin_relu_p_kernel(
         def product(codes, plane, picked, d, c):
             bank = psum.tile([P, PACK, CHUNK], F32, name="bank")
             for t in range(PACK):
-                cols = slice(t * P, (t + 1) * P)
+                cols = slice(t % 2 * P, (t % 2 + 1) * P)
                 nc.tensor.matmul_mx(
                     out=bank[:, t, :],
-                    lhsT=codes[:, cols].bitcast(FP8X4),
-                    lhsT_scale=plane[:, cols],
+                    lhsT=codes[t // 2][:, cols].bitcast(FP8X4),
+                    lhsT_scale=plane[t // 2][:, cols],
                     rhs=picked[:, c * CHUNK : (c + 1) * CHUNK].bitcast(FP8X4),
                     rhs_scale=picked_scales[:, d * V + c * CHUNK : d * V + (c + 1) * CHUNK],
                     start=True,
@@ -117,11 +116,12 @@ def tile_picked_trilin_relu_p_kernel(
         def chunk_tile(slot):
             return tile([P, CHUNK, PACK], F32, slot)
 
-        planes = [tile([P, H], U8, f"plane{d}") for d in range(3)]
+        planes = [[tile([P, H // 2], U8, f"plane{d}_{half}")[:] for half in range(2)] for d in range(3)]
 
         rounded1 = [half_tile("rounded1a"), half_tile("rounded1b")]
         rounded2 = [half_tile("rounded2a"), half_tile("rounded2b")]
-        codes1 = tile([P, H], U32, "table_scales")
+        both = tile([P, 2, H // 2], U32, "table_scales")
+        codes1 = [both[:, 0], both[:, 1]]
         for half in range(2):
             round_weight(nc.scalar.copy, 0, rounded1, half)
         for half in range(2):
@@ -129,15 +129,14 @@ def tile_picked_trilin_relu_p_kernel(
         picked12 = tile([P, 2, V], U32, "rounded1b")
         gather_words(picked12[:, 0], 0)
         gather_words(picked12[:, 1], 1)
-        for half in range(2):
-            round_weight(nc.scalar.copy, 1, rounded2, half, js=slice(0, 2))
+        round_weight(nc.scalar.copy, 1, rounded2, 0, js=slice(0, 2))
         y1 = [chunk_tile(f"y1_{c}") for c in range(CHUNKS)]
         for c in range(CHUNKS):
             nc.scalar.copy(out=y1[c][:], in_=product(codes1, planes[0], picked12[:, 0], 0, c))
 
-        codes2 = tile([P, H], U32, "codes2")
-        for half in range(2):
-            round_weight(nc.vector.tensor_copy, 1, rounded2, half, js=slice(2, PACK))
+        codes2 = [tile([P, H // 2], U32, f"codes2_{half}")[:] for half in range(2)]
+        round_weight(nc.vector.tensor_copy, 1, rounded2, 0, js=slice(2, PACK))
+        round_weight(nc.vector.tensor_copy, 1, rounded2, 1)
         for half in range(2):
             quantize_half(codes2, planes[1], rounded2, half)
         picked3 = tile([P, V], U32, "rounded2a")
@@ -147,7 +146,7 @@ def tile_picked_trilin_relu_p_kernel(
             return product(codes2, planes[1], picked12[:, 1], 1, c)
 
         rounded3 = [half_tile("rounded3a"), half_tile("rounded3b")]
-        codes3 = tile([P, H], U32, "codes3")
+        codes3 = [tile([P, H // 2], U32, f"codes3_{half}")[:] for half in range(2)]
         round_weight(nc.scalar.copy, 2, rounded3, 0)
         round_weight(nc.scalar.copy, 2, rounded3, 1, ms=slice(0, SCALAR_W3_SHARE))
         round_weight(gpsimd_round, 2, rounded3, 1, ms=slice(SCALAR_W3_SHARE, P))

@@ -22,7 +22,7 @@ BLOCKS = K // 32
 CHUNK = 128
 CHUNKS = V // CHUNK
 PSUM_BANKS = 8
-TABLE_HEAD = 1024
+TABLE_HEAD = 768
 SCALAR_W3_SHARE = 48
 PIECES = ((0, 128), (128, 256), (256, 384), (384, 448), (448, 512))
 
@@ -55,8 +55,8 @@ def tile_picked_trilin_relu_p_kernel(
         nc.sync.dma_start(out=table_words[:, :TABLE_HEAD], in_=words_hbm[:, :TABLE_HEAD])
         nc.sync.dma_start(offsets[:], offs)
         nc.sync.dma_start(out=table_scales[11 : 11 + 7 * BLOCKS : 7, :].bitcast(I32), in_=x_scales[0].bitcast(I32))
-        nc.sync.dma_start(out=raw[0][:], in_=w_rows[0])
         nc.sync.dma_start(out=table_words[:, TABLE_HEAD:], in_=words_hbm[:, TABLE_HEAD:])
+        nc.sync.dma_start(out=raw[0][:], in_=w_rows[0])
         nc.sync.dma_start(out=raw[1][:, :2], in_=w_rows[1][:, :2])
         nc.vector.tensor_copy(spread_scales[:], table_scales[:].indirect(offsets[:]))
 
@@ -119,24 +119,26 @@ def tile_picked_trilin_relu_p_kernel(
         planes = [[tile([P, H // 2], U8, f"plane{d}_{half}")[:] for half in range(2)] for d in range(3)]
 
         rounded1 = [half_tile("rounded1a"), half_tile("rounded1b")]
-        rounded2 = [half_tile("rounded2a"), half_tile("rounded2b")]
+        rounded2 = [half_tile("rounded2a"), None]
         both = tile([P, 2, H // 2], U32, "table_scales")
         codes1 = [both[:, 0], both[:, 1]]
-        for half in range(2):
-            round_weight(nc.scalar.copy, 0, rounded1, half)
-        for half in range(2):
-            quantize_half(codes1, planes[0], rounded1, half)
-        picked12 = tile([P, 2, V], U32, "rounded1b")
+        picked12 = tile([P, 2, V], U32, "picked12")
         gather_words(picked12[:, 0], 0)
         gather_words(picked12[:, 1], 1)
+        round_weight(nc.vector.tensor_copy, 0, rounded1, 0)
+        round_weight(nc.scalar.copy, 0, rounded1, 1)
+        for half in range(2):
+            quantize_half(codes1, planes[0], rounded1, half)
         round_weight(nc.scalar.copy, 1, rounded2, 0, js=slice(0, 2))
+        rounded2 = [rounded2[0], half_tile("raw0")]
+        round_weight(nc.vector.tensor_copy, 1, rounded2, 1, js=slice(0, 2))
         y1 = [chunk_tile(f"y1_{c}") for c in range(CHUNKS)]
         for c in range(CHUNKS):
             nc.scalar.copy(out=y1[c][:], in_=product(codes1, planes[0], picked12[:, 0], 0, c))
 
         codes2 = [tile([P, H // 2], U32, f"codes2_{half}")[:] for half in range(2)]
-        round_weight(nc.vector.tensor_copy, 1, rounded2, 0, js=slice(2, PACK))
-        round_weight(nc.vector.tensor_copy, 1, rounded2, 1)
+        for half in range(2):
+            round_weight(nc.vector.tensor_copy, 1, rounded2, half, js=slice(2, PACK))
         for half in range(2):
             quantize_half(codes2, planes[1], rounded2, half)
         picked3 = tile([P, V], U32, "rounded2a")

@@ -24,6 +24,7 @@ CHUNKS = V // CHUNK
 PSUM_BANKS = 8
 TABLE_HEAD = 768
 SCALAR_W3_SHARE = 48
+SCALAR_W1_SHARE = 112
 PIECES = ((0, 128), (128, 256), (256, 384), (384, 448), (448, 512))
 
 
@@ -94,24 +95,26 @@ def tile_picked_trilin_relu_p_kernel(
                 in_=rounded[half][:].rearrange("p t m j -> p (t m j)"),
             )
 
-        def gather_words(picked, d):
-            piece = offsets[:, d * V // 16 : (d + 1) * V // 16]
+        def gather_words(picked, first, end):
+            piece = offsets[:, first * V // 16 : end * V // 16]
             nc.vector.tensor_copy(picked, table_words[:].bitcast(U32).indirect(piece))
 
         def product(codes, plane, picked, d, c):
             bank = psum.tile([P, PACK, CHUNK], F32, name="bank")
             for t in range(PACK):
-                cols = slice(t % 2 * P, (t % 2 + 1) * P)
                 nc.tensor.matmul_mx(
                     out=bank[:, t, :],
-                    lhsT=codes[t // 2][:, cols].bitcast(FP8X4),
-                    lhsT_scale=plane[t // 2][:, cols],
+                    lhsT=codes[t].bitcast(FP8X4),
+                    lhsT_scale=plane[t],
                     rhs=picked[:, c * CHUNK : (c + 1) * CHUNK].bitcast(FP8X4),
                     rhs_scale=picked_scales[:, d * V + c * CHUNK : d * V + (c + 1) * CHUNK],
                     start=True,
                     stop=True,
                 )
             return bank[:].rearrange("p t v -> p v t")
+
+        def by_t(halves):
+            return [halves[t // 2][:, t % 2 * P : (t % 2 + 1) * P] for t in range(PACK)]
 
         def chunk_tile(slot):
             return tile([P, CHUNK, PACK], F32, slot)
@@ -123,10 +126,10 @@ def tile_picked_trilin_relu_p_kernel(
         both = tile([P, 2, H // 2], U32, "table_scales")
         codes1 = [both[:, 0], both[:, 1]]
         picked12 = tile([P, 2, V], U32, "picked12")
-        gather_words(picked12[:, 0], 0)
-        gather_words(picked12[:, 1], 1)
+        gather_words(picked12[:].rearrange("p d v -> p (d v)"), 0, 2)
         round_weight(nc.vector.tensor_copy, 0, rounded1, 0)
-        round_weight(nc.scalar.copy, 0, rounded1, 1)
+        round_weight(nc.vector.tensor_copy, 0, rounded1, 1, ms=slice(SCALAR_W1_SHARE, P))
+        round_weight(nc.scalar.copy, 0, rounded1, 1, ms=slice(0, SCALAR_W1_SHARE))
         for half in range(2):
             quantize_half(codes1, planes[0], rounded1, half)
         round_weight(nc.scalar.copy, 1, rounded2, 0, js=slice(0, 2))
@@ -134,7 +137,7 @@ def tile_picked_trilin_relu_p_kernel(
         round_weight(nc.vector.tensor_copy, 1, rounded2, 1, js=slice(0, 2))
         y1 = [chunk_tile(f"y1_{c}") for c in range(CHUNKS)]
         for c in range(CHUNKS):
-            nc.scalar.copy(out=y1[c][:], in_=product(codes1, planes[0], picked12[:, 0], 0, c))
+            nc.scalar.copy(out=y1[c][:], in_=product(by_t(codes1), by_t(planes[0]), picked12[:, 0], 0, c))
 
         codes2 = [tile([P, H // 2], U32, f"codes2_{half}")[:] for half in range(2)]
         for half in range(2):
@@ -142,10 +145,10 @@ def tile_picked_trilin_relu_p_kernel(
         for half in range(2):
             quantize_half(codes2, planes[1], rounded2, half)
         picked3 = tile([P, V], U32, "rounded2a")
-        gather_words(picked3[:], 2)
+        gather_words(picked3[:], 2, 3)
 
         def second_factor(c):
-            return product(codes2, planes[1], picked12[:, 1], 1, c)
+            return product(by_t(codes2), by_t(planes[1]), picked12[:, 1], 1, c)
 
         rounded3 = [half_tile("rounded3a"), half_tile("rounded3b")]
         codes3 = [tile([P, H // 2], U32, f"codes3_{half}")[:] for half in range(2)]
@@ -155,8 +158,16 @@ def tile_picked_trilin_relu_p_kernel(
         y12 = [chunk_tile("y12_0")[:], chunk_tile("y12_1")[:]]
         for c in range(2):
             nc.vector.tensor_tensor(y12[c], second_factor(c), y1[c][:], MULT)
-        for half in range(2):
-            quantize_half(codes3, planes[2], rounded3, half)
+        quantize_half(codes3, planes[2], rounded3, 0)
+        codes3_t, plane3_t = by_t(codes3)[:2], by_t(planes[2])[:2]
+        for t in (2, 3):
+            codes3_t.append(tile([P, P], U32, f"codes3_t{t}")[:])
+            plane3_t.append(tile([P, P], U8, f"plane3_t{t}")[:])
+            nc.vector.quantize_mx(
+                out=codes3_t[t].bitcast(FP8X4),
+                scales=plane3_t[t],
+                in_=rounded3[1][:, t - 2].rearrange("p m j -> p (m j)"),
+            )
         after_rounding = tile([P, 2, CHUNK, PACK], F32, "raw2")
         y2_last = after_rounding[:, 1]
         y12.extend([after_rounding[:, 0], chunk_tile("rounded3b")[:]])
@@ -165,7 +176,7 @@ def tile_picked_trilin_relu_p_kernel(
         nc.gpsimd.tensor_tensor(y12[3], y2_last, y1[3][:], MULT)
 
         z = tile([P, V, PACK], BF16, "z")
-        y3 = [product(codes3, planes[2], picked3, 2, c) for c in range(CHUNKS)]
+        y3 = [product(codes3_t, plane3_t, picked3, 2, c) for c in range(CHUNKS)]
 
         def multiply_piece(v0, v1):
             c, first = divmod(v0, CHUNK)

@@ -183,19 +183,20 @@ def tile_picked_trilin_relu_p_kernel(
             inside = slice(first, first + v1 - v0)
             nc.vector.tensor_tensor(z[:, v0:v1], y3[c][:, inside], y12[c][:, inside], MULT)
 
+        results = [tile([P, N // P, CHUNK], F32, f"result{c}") for c in range(CHUNKS)]
+
         def finish_piece(v0, v1):
             width = v1 - v0
             z_codes = tile([P, width], U32, f"z_codes{v0}")
             z_plane = tile([P, width], U8, f"z_plane{v0}")
-            result = tile([P, N // P, width], F32, f"result{v0}")
             nc.vector.quantize_mx(
                 out=z_codes[:].bitcast(FP8X4), scales=z_plane[:], in_=z[:, v0:v1].rearrange("p v t -> p (v t)")
             )
-            bank = psum.tile([P, PACK, CHUNK], F32, name="bank")
-            for h in range(N // P):
+
+            def last_product(bank, h):
                 cols = slice(h * P, (h + 1) * P)
                 nc.tensor.matmul_mx(
-                    out=bank[:, h, :width],
+                    out=bank,
                     lhsT=w4_codes[:, cols].bitcast(FP8X4),
                     lhsT_scale=w4_plane[:, cols],
                     rhs=z_codes[:].bitcast(FP8X4),
@@ -203,9 +204,23 @@ def tile_picked_trilin_relu_p_kernel(
                     start=True,
                     stop=True,
                 )
-            nc.scalar.activation(out=result[:], in_=bank[:, : N // P, :width], func=RELU)
-            queue = nc.scalar if v1 == V else nc.sync
-            queue.dma_start(out=out[:, v0:v1].rearrange("(h p) v -> p h v", p=P), in_=result[:])
+
+            c, first = divmod(v0, CHUNK)
+            result = results[c][:, :, first : first + width]
+            rows = out[:, c * CHUNK : (c + 1) * CHUNK].rearrange("(h p) v -> p h v", p=P)
+            if v1 < V:
+                bank = psum.tile([P, PACK, CHUNK], F32, name="bank")
+                for h in range(N // P):
+                    last_product(bank[:, h, :width], h)
+                nc.scalar.activation(out=result, in_=bank[:, : N // P, :width], func=RELU)
+                if v1 % CHUNK == 0:
+                    nc.sync.dma_start(out=rows, in_=results[c][:])
+            else:
+                for h, queue in enumerate((nc.sync, nc.scalar)):
+                    bank = psum.tile([P, PACK, CHUNK], F32, name="bank")
+                    last_product(bank[:, 0, :width], h)
+                    nc.scalar.activation(out=result[:, h], in_=bank[:, 0, :width], func=RELU)
+                    queue.dma_start(out=rows[:, h], in_=results[c][:, h])
 
         for before, piece in zip((None,) + PIECES, PIECES + (None,)):
             if piece is not None:

@@ -24,7 +24,7 @@ CHUNKS = V // CHUNK
 PSUM_BANKS = 8
 TABLE_HEAD = 768
 SCALAR_W3_SHARE = 48
-SCALAR_W1_SHARE = 112
+SCALAR_W1_SHARES = (48, 64)
 PIECES = ((0, 128), (128, 256), (256, 384), (384, 448), (448, 512))
 
 
@@ -127,9 +127,9 @@ def tile_picked_trilin_relu_p_kernel(
         codes1 = [both[:, 0], both[:, 1]]
         picked12 = tile([P, 2, V], U32, "picked12")
         gather_words(picked12[:].rearrange("p d v -> p (d v)"), 0, 2)
-        round_weight(nc.vector.tensor_copy, 0, rounded1, 0)
-        round_weight(nc.vector.tensor_copy, 0, rounded1, 1, ms=slice(SCALAR_W1_SHARE, P))
-        round_weight(nc.scalar.copy, 0, rounded1, 1, ms=slice(0, SCALAR_W1_SHARE))
+        for half, share in enumerate(SCALAR_W1_SHARES):
+            round_weight(nc.scalar.copy, 0, rounded1, half, ms=slice(0, share))
+            round_weight(nc.vector.tensor_copy, 0, rounded1, half, ms=slice(share, P))
         for half in range(2):
             quantize_half(codes1, planes[0], rounded1, half)
         round_weight(nc.scalar.copy, 1, rounded2, 0, js=slice(0, 2))

@@ -24,7 +24,7 @@ CHUNKS = V // CHUNK
 PSUM_BANKS = 8
 TABLE_HEAD = 768
 SCALAR_W3_SHARE = 48
-SCALAR_W1_SHARES = (48, 64)
+SCALAR_W1_SHARES = (40, 56)
 PIECES = ((0, 128), (128, 256), (256, 384), (384, 448), (448, 512))
 
 

from contextlib import ExitStack

import concourse.mybir as mybir

K, T, S, V, H, N = 512, 4096, 1536, 512, 512, 256
FLOPS = 2 * 3 * K * H * V + 2 * H * N * V

F32 = mybir.dt.float32
BF16 = mybir.dt.bfloat16
I32 = mybir.dt.int32
U32 = mybir.dt.uint32
U16 = mybir.dt.uint16
U8 = mybir.dt.uint8
FP8X4 = mybir.dt.float8_e4m3fn_x4
MULT = mybir.AluOpType.mult
ADD = mybir.AluOpType.add
RELU = mybir.ActivationFunctionType.Relu

P = 128
PACK = 4
BLOCKS = K // 32
CHUNK = 128
CHUNKS = V // CHUNK
PSUM_BANKS = 8
TABLE_HEAD = 768
SCALAR_W3_SHARE = 48
SCALAR_W1_SHARES = (40, 56)
PIECES = ((0, 128), (128, 256), (256, 384), (384, 448), (448, 512))


def tile_picked_trilin_relu_p_kernel(
    tc, x_words, x_scales, w1, w2, w3, w4_words, w4_scales, offs, out
):
    nc = tc.nc
    with ExitStack() as ctx:
        keep = ctx.enter_context(tc.tile_pool(name="keep", bufs=1))
        psum = ctx.enter_context(tc.psum_pool(name="psum", bufs=PSUM_BANKS))

        def tile(shape, dtype, slot):
            return keep.tile(shape, dtype, name=slot, align_bytes=64)

        offsets = keep.tile([P, S // 16], U16, name="offsets")
        table_words = tile([P, T], I32, "table_words")
        table_scales = tile([P, T], U8, "table_scales")
        raw = [tile([P, PACK, H], F32, f"raw{d}") for d in range(3)]
        w4_codes = tile([P, N], I32, "w4_codes")
        w4_plane = tile([P, N], U8, "w4_plane")
        spread_scales = tile([P, S], U8, "spread_scales")
        picked_scales = tile([P, S], U8, "picked_scales")

        nc.vector.memset(table_scales[:].bitcast(I32), 0)
        nc.vector.memset(w4_plane[:].bitcast(I32), 0)
        nc.vector.memset(picked_scales[:].bitcast(I32), 0)
        words_hbm = x_words[0].rearrange("p n j -> p (n j)").bitcast(I32)
        w_rows = [w.rearrange("(p j) i -> p j i", j=PACK) for w in (w1, w2, w3)]
        nc.sync.dma_start(out=table_words[:, :TABLE_HEAD], in_=words_hbm[:, :TABLE_HEAD])
        nc.sync.dma_start(offsets[:], offs)
        nc.sync.dma_start(out=table_scales[11 : 11 + 7 * BLOCKS : 7, :].bitcast(I32), in_=x_scales[0].bitcast(I32))
        nc.sync.dma_start(out=table_words[:, TABLE_HEAD:], in_=words_hbm[:, TABLE_HEAD:])
        nc.sync.dma_start(out=raw[0][:], in_=w_rows[0])
        nc.sync.dma_start(out=raw[1][:, :2], in_=w_rows[1][:, :2])
        nc.vector.tensor_copy(spread_scales[:], table_scales[:].indirect(offsets[:]))

        def move_scales(cols):
            for r in range(4):
                nc.sync.dma_start(
                    out=picked_scales[r:P:32, cols].bitcast(I32),
                    in_=spread_scales[11 + 7 * r : 11 + 7 * BLOCKS : 28, cols].bitcast(I32),
                )

        move_scales(slice(0, 2 * V))
        nc.sync.dma_start(out=raw[1][:, 2:], in_=w_rows[1][:, 2:])
        nc.sync.dma_start(out=raw[2][:], in_=w_rows[2])
        move_scales(slice(2 * V, S))
        nc.sync.dma_start(out=w4_codes[:], in_=w4_words[0].rearrange("p n j -> p (n j)").bitcast(I32))
        for r in range(4):
            nc.sync.dma_start(out=w4_plane[r:P:32, :].bitcast(I32), in_=w4_scales[0, r:BLOCKS:4, :].bitcast(I32))

        def half_tile(slot):
            return tile([P, 2, P, PACK], BF16, slot)

        def round_weight(copy, d, rounded, half, ms=slice(0, P), js=slice(0, PACK)):
            src = raw[d][:].rearrange("p j (m t) -> p m j t", t=PACK)[:, ms, js, 2 * half : 2 * half + 2]
            copy(out=rounded[half][:].rearrange("p t m j -> p m j t")[:, ms, js, :], in_=src)

        def gpsimd_round(out, in_):
            nc.gpsimd.tensor_scalar(
                out.rearrange("p m j t -> p m t j"), in_.rearrange("p m j t -> p m t j"), 1.0, 0.0, MULT, ADD
            )

        def quantize_half(codes, plane, rounded, half):
            nc.vector.quantize_mx(
                out=codes[half].bitcast(FP8X4),
                scales=plane[half],
                in_=rounded[half][:].rearrange("p t m j -> p (t m j)"),
            )

        def gather_words(picked, first, end):
            piece = offsets[:, first * V // 16 : end * V // 16]
            nc.vector.tensor_copy(picked, table_words[:].bitcast(U32).indirect(piece))

        def product(codes, plane, picked, d, c):
            bank = psum.tile([P, PACK, CHUNK], F32, name="bank")
            for t in range(PACK):
                nc.tensor.matmul_mx(
                    out=bank[:, t, :],
                    lhsT=codes[t].bitcast(FP8X4),
                    lhsT_scale=plane[t],
                    rhs=picked[:, c * CHUNK : (c + 1) * CHUNK].bitcast(FP8X4),
                    rhs_scale=picked_scales[:, d * V + c * CHUNK : d * V + (c + 1) * CHUNK],
                    start=True,
                    stop=True,
                )
            return bank[:].rearrange("p t v -> p v t")

        def by_t(halves):
            return [halves[t // 2][:, t % 2 * P : (t % 2 + 1) * P] for t in range(PACK)]

        def chunk_tile(slot):
            return tile([P, CHUNK, PACK], F32, slot)

        planes = [[tile([P, H // 2], U8, f"plane{d}_{half}")[:] for half in range(2)] for d in range(3)]

        rounded1 = [half_tile("rounded1a"), half_tile("rounded1b")]
        rounded2 = [half_tile("rounded2a"), None]
        both = tile([P, 2, H // 2], U32, "table_scales")
        codes1 = [both[:, 0], both[:, 1]]
        picked12 = tile([P, 2, V], U32, "picked12")
        gather_words(picked12[:].rearrange("p d v -> p (d v)"), 0, 2)
        for half, share in enumerate(SCALAR_W1_SHARES):
            round_weight(nc.scalar.copy, 0, rounded1, half, ms=slice(0, share))
            round_weight(nc.vector.tensor_copy, 0, rounded1, half, ms=slice(share, P))
        for half in range(2):
            quantize_half(codes1, planes[0], rounded1, half)
        round_weight(nc.scalar.copy, 1, rounded2, 0, js=slice(0, 2))
        rounded2 = [rounded2[0], half_tile("raw0")]
        round_weight(nc.vector.tensor_copy, 1, rounded2, 1, js=slice(0, 2))
        y1 = [chunk_tile(f"y1_{c}") for c in range(CHUNKS)]
        for c in range(CHUNKS):
            nc.scalar.copy(out=y1[c][:], in_=product(by_t(codes1), by_t(planes[0]), picked12[:, 0], 0, c))

        codes2 = [tile([P, H // 2], U32, f"codes2_{half}")[:] for half in range(2)]
        for half in range(2):
            round_weight(nc.vector.tensor_copy, 1, rounded2, half, js=slice(2, PACK))
        for half in range(2):
            quantize_half(codes2, planes[1], rounded2, half)
        picked3 = tile([P, V], U32, "rounded2a")
        gather_words(picked3[:], 2, 3)

        def second_factor(c):
            return product(by_t(codes2), by_t(planes[1]), picked12[:, 1], 1, c)

        rounded3 = [half_tile("rounded3a"), half_tile("rounded3b")]
        codes3 = [tile([P, H // 2], U32, f"codes3_{half}")[:] for half in range(2)]
        round_weight(nc.scalar.copy, 2, rounded3, 0)
        round_weight(nc.scalar.copy, 2, rounded3, 1, ms=slice(0, SCALAR_W3_SHARE))
        round_weight(gpsimd_round, 2, rounded3, 1, ms=slice(SCALAR_W3_SHARE, P))
        y12 = [chunk_tile("y12_0")[:], chunk_tile("y12_1")[:]]
        for c in range(2):
            nc.vector.tensor_tensor(y12[c], second_factor(c), y1[c][:], MULT)
        quantize_half(codes3, planes[2], rounded3, 0)
        codes3_t, plane3_t = by_t(codes3)[:2], by_t(planes[2])[:2]
        for t in (2, 3):
            codes3_t.append(tile([P, P], U32, f"codes3_t{t}")[:])
            plane3_t.append(tile([P, P], U8, f"plane3_t{t}")[:])
            nc.vector.quantize_mx(
                out=codes3_t[t].bitcast(FP8X4),
                scales=plane3_t[t],
                in_=rounded3[1][:, t - 2].rearrange("p m j -> p (m j)"),
            )
        after_rounding = tile([P, 2, CHUNK, PACK], F32, "raw2")
        y2_last = after_rounding[:, 1]
        y12.extend([after_rounding[:, 0], chunk_tile("rounded3b")[:]])
        nc.vector.tensor_tensor(y12[2], second_factor(2), y1[2][:], MULT)
        nc.scalar.copy(out=y2_last, in_=second_factor(3))
        nc.gpsimd.tensor_tensor(y12[3], y2_last, y1[3][:], MULT)

        z = tile([P, V, PACK], BF16, "z")
        y3 = [product(codes3_t, plane3_t, picked3, 2, c) for c in range(CHUNKS)]

        def multiply_piece(v0, v1):
            c, first = divmod(v0, CHUNK)
            inside = slice(first, first + v1 - v0)
            nc.vector.tensor_tensor(z[:, v0:v1], y3[c][:, inside], y12[c][:, inside], MULT)

        results = [tile([P, N // P, CHUNK], F32, f"result{c}") for c in range(CHUNKS)]

        def finish_piece(v0, v1):
            width = v1 - v0
            z_codes = tile([P, width], U32, f"z_codes{v0}")
            z_plane = tile([P, width], U8, f"z_plane{v0}")
            nc.vector.quantize_mx(
                out=z_codes[:].bitcast(FP8X4), scales=z_plane[:], in_=z[:, v0:v1].rearrange("p v t -> p (v t)")
            )

            def last_product(bank, h):
                cols = slice(h * P, (h + 1) * P)
                nc.tensor.matmul_mx(
                    out=bank,
                    lhsT=w4_codes[:, cols].bitcast(FP8X4),
                    lhsT_scale=w4_plane[:, cols],
                    rhs=z_codes[:].bitcast(FP8X4),
                    rhs_scale=z_plane[:],
                    start=True,
                    stop=True,
                )

            c, first = divmod(v0, CHUNK)
            result = results[c][:, :, first : first + width]
            rows = out[:, c * CHUNK : (c + 1) * CHUNK].rearrange("(h p) v -> p h v", p=P)
            if v1 < V:
                bank = psum.tile([P, PACK, CHUNK], F32, name="bank")
                for h in range(N // P):
                    last_product(bank[:, h, :width], h)
                nc.scalar.activation(out=result, in_=bank[:, : N // P, :width], func=RELU)
                if v1 % CHUNK == 0:
                    nc.sync.dma_start(out=rows, in_=results[c][:])
            else:
                for h, queue in enumerate((nc.sync, nc.scalar)):
                    bank = psum.tile([P, PACK, CHUNK], F32, name="bank")
                    last_product(bank[:, 0, :width], h)
                    nc.scalar.activation(out=result[:, h], in_=bank[:, 0, :width], func=RELU)
                    queue.dma_start(out=rows[:, h], in_=results[c][:, h])

        for before, piece in zip((None,) + PIECES, PIECES + (None,)):
            if piece is not None:
                multiply_piece(*piece)
            if before is not None:
                finish_piece(*before)
